import numpy as np
import ml_dtypes


def mxq(x, axis, fmt="e4m3"):
    dtype, down = {"e4m3": (ml_dtypes.float8_e4m3fn, 7), "e5m2": (ml_dtypes.float8_e5m2, 14)}[fmt]
    v = np.moveaxis(np.asarray(x, np.float32).astype(ml_dtypes.bfloat16).astype(np.float64), axis, -1)
    blocks = v.reshape(v.shape[:-1] + (-1, 32))
    amax = np.abs(blocks).max(-1, keepdims=True)
    byte = np.maximum(np.where(amax > 0, np.frexp(amax)[1] - 1 + 127, 0) - down, 1)
    scale = np.exp2(byte - 127.0)
    codes = (blocks / scale).astype(np.float32).astype(dtype).astype(np.float64)
    return np.moveaxis((codes * scale).reshape(v.shape), -1, axis)


WIDE = False


def mx_kscale(k):
    if not WIDE:
        return np.ones(k)
    levels = np.array([10, -10, 5, -5, 0])
    if k % 512:
        return np.exp2(np.random.permutation(np.resize(levels, k // 32))).repeat(32)
    a = np.empty((k // 512, 16))
    for p in range(k // 512):
        a[p, :8] = np.random.permutation(np.resize(levels, 8))
        for g in range(8):
            far = levels[np.abs(levels - a[p, g]) >= 10]
            a[p, g + 8] = far[np.random.randint(len(far))]
    return np.exp2(a.ravel()).repeat(32)


BF16 = ml_dtypes.bfloat16


def bf(x):
    return np.asarray(x, np.float32).astype(BF16)


def f64(x):
    return np.asarray(x).astype(np.float64)


E2M1 = np.array([0.0, 0.5, 1.0, 1.5, 2.0, 3.0, 4.0, 6.0, -0.0, -0.5, -1.0, -1.5, -2.0, -3.0, -4.0, -6.0])


def pack_weight(w, fmt):
    k, n = w.shape
    w = f64(bf(w)).reshape(k // 32, 32, n)
    amax = np.abs(w).max(1)
    if fmt == "e4m3":
        byte = np.frexp(amax)[1] - 1 + 127 - 7
    else:
        mant, ex = np.frexp(amax / 6.0)
        byte = np.where(mant > 0.5, ex, ex - 1) + 127
    byte = np.clip(np.where(amax > 0, byte, 1), 1, 254)
    scaled = (w * np.exp2(127.0 - byte)[:, None, :]).reshape(k, n).astype(np.float32)
    by_word = np.ascontiguousarray(scaled.reshape(k // 512, 128, 4, n).transpose(0, 1, 3, 2))
    if fmt == "e4m3":
        words = by_word.astype(ml_dtypes.float8_e4m3fn).view(np.uint8)
    else:
        c = by_word.astype(ml_dtypes.float4_e2m1fn).view(np.uint8) & 0xF
        words = c[..., 0::2] | (c[..., 1::2] << 4)
    return np.ascontiguousarray(words), np.ascontiguousarray(byte.astype(np.uint8).reshape(k // 512, 16, n))


def unpack_weight(words, scales, fmt):
    g, p, n, _ = words.shape
    if fmt == "e4m3":
        vals = np.ascontiguousarray(words).view(ml_dtypes.float8_e4m3fn).astype(np.float64)
    else:
        nib = np.empty((g, p, n, 4), np.uint8)
        nib[..., 0::2] = words & 0xF
        nib[..., 1::2] = words >> 4
        vals = E2M1[nib]
    vals = vals * np.repeat(np.exp2(scales.astype(np.float64) - 127.0), 8, axis=1)[..., None]
    return vals.transpose(0, 1, 3, 2).reshape(g * 512, n)
def pack4(w):
    words, scales = pack_weight(w, "e2m1")
    return words.reshape(words.shape[0], 128, -1), scales


def unpack4(words, scales):
    return unpack_weight(words.reshape(words.shape[0], 128, -1, 2), scales, "e2m1")


def planes(Y):
    n, m = Y.shape
    b = f64(bf(Y)).reshape(n // 32, 32, m)
    amax = np.abs(b).max(1)
    byte = np.clip(np.where(amax > 0, np.frexp(amax)[1] - 1 + 127 - 7, 1), 1, 254)
    codes = (b * np.exp2(127.0 - byte)[:, None, :]).reshape(n, m).astype(np.float32).astype(ml_dtypes.float8_e4m3fn).view(np.uint8)
    words = codes.reshape(n // 512, 128, 4, m).transpose(0, 1, 3, 2)
    return np.ascontiguousarray(words), np.ascontiguousarray(byte.astype(np.uint8).reshape(n // 512, 16, m))


C, D, E, R = 2048, 1024, 1536, 1024

def setup_inputs():
    s = mx_kscale(C)
    t = mx_kscale(D)
    u = np.exp(0.8 * np.random.randn(E))
    x = np.random.randn(C, D) / np.sqrt(C) * s[:, None] * t[None, :]
    v = np.random.randn(C, E) * u[None, :] / s[:, None]
    x_words, x_scales = pack_weight(x, "e4m3")
    v_words, v_scales = pack4(v)
    return {
        "x_words": x_words, "x_scales": x_scales,
        "v_words": v_words, "v_scales": v_scales,
        "state": bf(0.8 * np.random.randn(D, E) * u[None, :] * t[:, None]),
        "decay": bf(np.exp(-np.random.rand(D))),
        "queries": bf(np.random.randn(R, D) / np.sqrt(D) / t[None, :]),
        "local_part": bf(0.7 * np.random.randn(R, E) * u[None, :]),
        "gate": bf(1.5 * np.random.randn(R, E)),
    }

def reference(x_words, x_scales, v_words, v_scales, state, decay, queries, local_part, gate):
    X = unpack_weight(x_words, x_scales, "e4m3")
    V = unpack4(v_words, v_scales)
    H = X.T @ V
    S = f64(decay)[:, None] * (f64(state) + H)
    O = mxq(f64(queries), 1, "e4m3") @ mxq(S, 0, "e4m3")
    G = f64(gate)
    y = (f64(local_part) + O) * (G / (1.0 + np.exp(-G)))
    Y = y.T
    words, scales = planes(Y)
    return y, words, scales

@@ -1,0 +1,409 @@
+from contextlib import ExitStack
+
+import concourse.mybir as mybir
+from concourse.masks import make_identity
+
+C, D, E, R = 2048, 1024, 1536, 1024
+FLOPS = 2 * C * D * E + 2 * R * D * E
+
+F32 = mybir.dt.float32
+BF16 = mybir.dt.bfloat16
+I32 = mybir.dt.int32
+U32 = mybir.dt.uint32
+U8 = mybir.dt.uint8
+FP8X4 = mybir.dt.float8_e4m3fn_x4
+FP4X4 = mybir.dt.float4_e2m1fn_x4
+ACT = mybir.ActivationFunctionType
+ALU = mybir.AluOpType
+
+P = 128
+PACK = 4
+KP = P * PACK
+TOKEN_PASSES = C // KP
+KEY_PASSES = D // KP
+CHUNKS = E // KP
+ROW_TILES = R // P
+STATE_UNITS = CHUNKS * KEY_PASSES * PACK
+OUT_UNITS = CHUNKS * ROW_TILES
+LEAD = 10
+SILU_AHEAD = 2
+
+
+def tile_decayed_state_read_h2_kernel(tc, x_words, x_scales, v_words, v_scales, state, decay, queries,
+                                                 local_part, gate, out_0, out_1, out_2):
+    nc = tc.nc
+    with ExitStack() as ctx:
+        keep = ctx.enter_context(tc.tile_pool(name="keep", bufs=1))
+        work = ctx.enter_context(tc.tile_pool(name="work", bufs=2))
+        psum = ctx.enter_context(tc.psum_pool(name="psum", bufs=2))
+        ctx.enter_context(tc.manual_schedule())
+
+        def big(name, dtype):
+            width = 4096 if dtype == BF16 else 2048
+            return work.tile([P, width], dtype, name=name, tag="big", bufs=4, align_bytes=64)
+
+        def interleaved(name, dtype):
+            width = 4096 if dtype == U8 else 2048
+            return work.tile([P, width], dtype, name=name, tag="interleaved", bufs=2, align_bytes=64)
+
+        warm = keep.tile([P, 8], F32, name="warm")
+        nc.vector.memset(warm[:], 0.0)
+        xs_raw = interleaved("xs_raw", U8)
+        nc.vector.memset(xs_raw[:].bitcast(I32), 0)
+        vs = keep.tile([P, TOKEN_PASSES * E], U8, name="vs", align_bytes=64)
+        nc.vector.memset(vs[:].bitcast(I32), 0)
+        warm_out = keep.tile([P, 8], F32, name="warm_out")
+        nc.scalar.activation(out=warm_out[:], in_=warm[:], func=ACT.Silu)
+
+        x_by_partition = x_words.rearrange("c p n t -> p c (n t)")
+        v_by_partition = v_words.rearrange("c p n -> p c n")
+        x_raw, v_codes, state_sb, q_sb, gate_sb, local_sb = {}, {}, {}, {}, {}, {}
+
+        def load_x(g, c0, c1):
+            if g not in x_raw:
+                x_raw[g] = big("x_raw%d" % g, I32)
+            nc.sync.dma_start(out=x_raw[g][:, KP * c0:KP * c1].rearrange("p (c n) -> p c n", n=KP),
+                              in_=x_by_partition[:, c0:c1, 4 * KP * g:4 * KP * (g + 1)].bitcast(I32))
+
+        def load_scales(queue, plane, scales, quads):
+            for quad in quads:
+                queue.dma_start(
+                    out=plane[32 * quad:32 * quad + 4, :].bitcast(I32).rearrange("p (c n) -> p c n", c=TOKEN_PASSES),
+                    in_=scales[:, 4 * quad:4 * quad + 4, :].rearrange("c r n -> r c n").bitcast(I32))
+
+        def load_v(j):
+            v_codes[j] = keep.tile([P, TOKEN_PASSES * 2 * KP], U8, name="v_codes%d" % j, align_bytes=64)
+            nc.sync.dma_start(out=v_codes[j][:].bitcast(I32).rearrange("p (c n) -> p c n", c=TOKEN_PASSES),
+                              in_=v_by_partition[:, :, 2 * KP * j:2 * KP * (j + 1)].bitcast(I32))
+
+        def load_state(j, g):
+            state_sb[j, g] = keep.tile([P, PACK * KP], BF16, name="state%d%d" % (j, g))
+            nc.sync.dma_start(
+                out=state_sb[j, g][:].rearrange("p (t e) -> p t e", t=PACK),
+                in_=state[KP * g:KP * (g + 1), KP * j:KP * (j + 1)].rearrange("(p t) e -> p t e", t=PACK))
+
+        def load_q(h):
+            q_sb[h] = big("q%d" % h, BF16)
+            nc.sync.dma_start(out=q_sb[h][:].rearrange("p (i d) -> p i d", i=4),
+                              in_=queries[KP * h:KP * (h + 1), :].rearrange("(i p) d -> p i d", p=P))
+
+        def load_rows(store, source, label, j, h):
+            store[j, h] = keep.tile([P, 4 * KP], BF16, name="%s%d%d" % (label, j, h))
+            nc.sync.dma_start(
+                out=store[j, h][:].rearrange("p (i e) -> p i e", i=4),
+                in_=source[KP * h:KP * (h + 1), KP * j:KP * (j + 1)].rearrange("(i p) e -> p i e", p=P))
+
+        def load_gate_local(j, h):
+            load_rows(gate_sb, gate, "gate", j, h)
+            load_rows(local_sb, local_part, "local", j, h)
+
+        load_scales(nc.gpsimd, vs, v_scales, (0, 1))
+        decay_bf = keep.tile([P, KEY_PASSES * PACK], BF16, name="decay_bf")
+        nc.gpsimd.dma_start(out=decay_bf[:].rearrange("p (g t) -> p g t", t=PACK),
+                            in_=decay.rearrange("(g p t) -> p g t", p=P, t=PACK))
+        ident = keep.tile([P, P], F32, name="ident")
+        make_identity(nc, ident[:])
+
+        load_x(0, 0, 2)
+        load_v(0)
+        load_scales(nc.sync, xs_raw, x_scales, range(4))
+        load_scales(nc.sync, vs, v_scales, (2, 3))
+        load_x(0, 2, 4)
+        load_x(1, 0, 2)
+        load_state(0, 0)
+        load_x(1, 2, 4)
+        load_state(0, 1)
+        load_q(0)
+        load_v(1)
+        load_state(1, 0)
+        load_gate_local(0, 0)
+        load_q(1)
+        load_gate_local(0, 1)
+        load_state(1, 1)
+        load_v(2)
+        load_state(2, 0)
+        load_gate_local(1, 0)
+        load_state(2, 1)
+        load_gate_local(1, 1)
+        load_gate_local(2, 0)
+        load_gate_local(2, 1)
+
+        x_codes, x_sc = {}, {}
+
+        def sort_x_scales(g, c0, c1):
+            if g not in x_sc:
+                x_sc[g] = keep.tile([P, TOKEN_PASSES * KP], U8, name="x_sc%d" % g, align_bytes=64)
+            src = xs_raw[:].rearrange("p (c n) -> p c n", c=TOKEN_PASSES)[:, c0:c1, KP * g:KP * (g + 1)]
+            nc.vector.tensor_copy(
+                out=x_sc[g][:, KP * c0:KP * c1].rearrange("p (c t a i) -> p c a t i", t=PACK, a=8, i=16),
+                in_=src.rearrange("p c (a i t) -> p c a t i", t=PACK, i=16))
+
+        def sort_x_codes(g, c0, c1):
+            if g not in x_codes:
+                x_codes[g] = keep.tile([P, TOKEN_PASSES * KP], I32, name="x_codes%d" % g, align_bytes=64)
+            cols = slice(KP * c0, KP * c1)
+            nc.vector.tensor_copy(
+                out=x_codes[g][:, cols].rearrange("p (c t a i) -> p c a t i", t=PACK, a=32, i=4),
+                in_=x_raw[g][:, cols].rearrange("p (c a i t) -> p c a t i", t=PACK, a=32, i=4))
+
+        decay_f = keep.tile([P, KEY_PASSES * PACK], F32, name="decay_f")
+
+        h_bank, decayed, s_rows, s_mixed, s_codes, s_scales = {}, {}, {}, {}, {}, {}
+
+        def unit(n):
+            return n // 8, n // 4 % 2, n % 4
+
+        def h_passes(n, c0, c1):
+            j, g, t = unit(n)
+            if c0 == 0:
+                h_bank[n] = psum.tile([P, KP], F32, name="h%d" % n, tag="acc", bufs=6)
+            for c in range(c0, c1):
+                cols = slice(KP * c + P * t, KP * c + P * (t + 1))
+                nc.tensor.matmul_mx(
+                    out=h_bank[n][:], lhsT=x_codes[g][:, cols].bitcast(FP8X4), lhsT_scale=x_sc[g][:, cols],
+                    rhs=v_codes[j][:, 2 * KP * c:2 * KP * (c + 1)].bitcast(FP4X4),
+                    rhs_scale=vs[:, E * c + KP * j:E * c + KP * (j + 1)],
+                    start=(c == 0), stop=(c == TOKEN_PASSES - 1))
+
+        def decay_state(n):
+            j, g, t = unit(n)
+            decayed[n] = work.tile([P, KP], F32, name="decayed%d" % n, tag="decayed", bufs=5)
+            nc.scalar.activation(out=decayed[n][:], in_=state_sb[j, g][:, KP * t:KP * (t + 1)], func=ACT.Copy,
+                                 scale=decay_f[:, PACK * g + t:PACK * g + t + 1])
+
+        def form_s(n):
+            j, g, t = unit(n)
+            if t == 0:
+                s_rows[j, g] = work.tile([P, PACK * KP], BF16, name="s_rows%d%d" % (j, g), tag="s_rows", bufs=2)
+            nc.vector.scalar_tensor_tensor(
+                out=s_rows[j, g][:, KP * t:KP * (t + 1)], in0=h_bank[n][:],
+                scalar=decay_f[:, PACK * g + t:PACK * g + t + 1], in1=decayed[n][:], op0=ALU.mult, op1=ALU.add)
+
+        def mix_s(j, g, copy, a0, a1):
+            if a0 == 0:
+                s_mixed[j, g] = interleaved("s_mixed%d%d" % (j, g), BF16)
+            copy(out=s_mixed[j, g][:].rearrange("p (a i t) -> p a t i", i=4, t=PACK)[:, a0:a1],
+                 in_=s_rows[j, g][:].rearrange("p (t a i) -> p a t i", i=4, t=PACK)[:, a0:a1])
+
+        def quantize_s(j, g):
+            s_codes[j, g] = work.tile([P, KP], U32, name="s_codes%d%d" % (j, g), tag="s_codes", bufs=4, align_bytes=64)
+            s_scales[j, g] = work.tile([P, KP], U8, name="s_scales%d%d" % (j, g), tag="s_scales", bufs=4,
+                                       align_bytes=64)
+            nc.vector.quantize_mx(out=s_codes[j, g][:].bitcast(FP8X4), scales=s_scales[j, g][:], in_=s_mixed[j, g][:])
+
+        q_bank, q_mixed, q_codes, q_scales = {}, {}, {}, {}
+
+        def turn_q(i):
+            q_bank[i] = psum.tile([P, KP], F32, name="q_bank%d" % i, tag="turn", bufs=2)
+            words = q_sb[i // 4][:].bitcast(F32)
+            for g in range(KEY_PASSES):
+                for u in range(2):
+                    first = KP * (i % 4) + 256 * g
+                    nc.tensor.transpose(q_bank[i][:, P * (2 * g + u):P * (2 * g + u + 1)],
+                                        words[:, first + u:first + 256:2], ident[:])
+
+        def copy_q(i):
+            if i % 2 == 0:
+                q_mixed[i // 2] = work.tile([P, 2048], BF16, name="q_mixed%d" % (i // 2), tag="q_mixed", bufs=2,
+                                            align_bytes=64)
+            words = q_mixed[i // 2][:].bitcast(F32)[:, KP * (i % 2):KP * (i % 2 + 1)]
+            nc.scalar.copy(out=words.rearrange("p (g r u) -> p g r u", g=KEY_PASSES, u=2),
+                           in_=q_bank[i][:].rearrange("p (g u r) -> p g r u", g=KEY_PASSES, u=2))
+
+        def quantize_q(a):
+            q_codes[a] = keep.tile([P, KP], U32, name="q_codes%d" % a, align_bytes=64)
+            q_scales[a] = keep.tile([P, KP], U8, name="q_scales%d" % a, align_bytes=64)
+            nc.vector.quantize_mx(out=q_codes[a][:].bitcast(FP8X4), scales=q_scales[a][:], in_=q_mixed[a][:])
+
+        o_bank, silu, summed, y_sb, y_bf, y_bank, y_mixed, y_codes, y_scales = {}, {}, {}, {}, {}, {}, {}, {}, {}
+
+        def o_passes(m):
+            j, i = divmod(m, ROW_TILES)
+            o_bank[m] = psum.tile([P, KP], F32, name="o%d" % m, tag="acc", bufs=6)
+            for g in range(KEY_PASSES):
+                cols = slice(P * (2 * (i % 2) + g), P * (2 * (i % 2) + g + 1))
+                nc.tensor.matmul_mx(
+                    out=o_bank[m][:], lhsT=q_codes[i // 2][:, cols].bitcast(FP8X4), lhsT_scale=q_scales[i // 2][:, cols],
+                    rhs=s_codes[j, g][:].bitcast(FP8X4), rhs_scale=s_scales[j, g][:],
+                    start=(g == 0), stop=(g == KEY_PASSES - 1))
+
+        def rows_of(store, m):
+            j, i = divmod(m, ROW_TILES)
+            return store[j, i // 4][:, KP * (i % 4):KP * (i % 4 + 1)]
+
+        def silu_gate(m):
+            silu[m] = work.tile([P, KP], F32, name="silu%d" % m, tag="silu", bufs=6)
+            nc.scalar.activation(out=silu[m][:], in_=rows_of(gate_sb, m), func=ACT.Silu)
+
+        def add_local(m):
+            summed[m] = work.tile([P, KP], F32, name="summed%d" % m, tag="summed", bufs=3)
+            nc.vector.tensor_tensor(out=summed[m][:], in0=o_bank[m][:], in1=rows_of(local_sb, m), op=ALU.add)
+
+        def y_rows(m):
+            return y_sb[m // 4][:, KP * (m % 4):KP * (m % 4 + 1)]
+
+        def apply_gate(m):
+            if m % 4 == 0:
+                y_sb[m // 4] = big("y%d" % (m // 4), F32)
+            nc.vector.tensor_tensor(out=y_rows(m), in0=summed[m][:], in1=silu[m][:], op=ALU.mult)
+
+        def store_y(m0, count):
+            j, i = divmod(m0, ROW_TILES)
+            nc.sync.dma_start(
+                out=out_0[P * i:P * (i + count), KP * j:KP * (j + 1)].rearrange("(i p) e -> p i e", p=P),
+                in_=y_sb[m0 // 4][:, KP * (m0 % 4):KP * (m0 % 4 + count)].rearrange("p (i e) -> p i e", e=KP))
+
+        def round_y(m, copy):
+            y_bf[m] = work.tile([P, KP], BF16, name="y_bf%d" % m, tag="y_bf", bufs=4)
+            copy(out=y_bf[m][:].rearrange("p (u a e) -> p u a e", u=2, e=2),
+                 in_=y_rows(m).rearrange("p (a u e) -> p u a e", u=2, e=2))
+
+        def turn_y(m0, count):
+            y_bank[m0] = psum.tile([P, KP], F32, name="y_bank%d" % m0, tag="turn", bufs=2)
+            for b in range(count):
+                words = y_bf[m0 + b][:].bitcast(F32)
+                for u in range(2):
+                    nc.tensor.transpose(y_bank[m0][:, P * (2 * b + u):P * (2 * b + u + 1)],
+                                        words[:, P * u:P * (u + 1)], ident[:])
+
+        def copy_y(m0, count):
+            y_mixed[m0] = work.tile([P, KP * count], BF16, name="y_mixed%d" % m0, tag="y_mixed", bufs=3, align_bytes=64)
+            nc.scalar.copy(out=y_mixed[m0][:].bitcast(F32).rearrange("p (b r u) -> p b r u", b=count, u=2),
+                           in_=y_bank[m0][:, :2 * P * count].rearrange("p (b u r) -> p b r u", b=count, u=2))
+
+        def quantize_y(m0, count):
+            j, i = divmod(m0, ROW_TILES)
+            if i == 0:
+                y_codes[j] = work.tile([P, R], U32, name="y_codes%d" % j, tag="y_codes", bufs=2, align_bytes=64)
+                y_scales[j] = keep.tile([P, R], U8, name="y_scales%d" % j, align_bytes=64)
+            cols = slice(P * i, P * (i + count))
+            nc.vector.quantize_mx(out=y_codes[j][:, cols].bitcast(FP8X4), scales=y_scales[j][:, cols],
+                                  in_=y_mixed[m0][:])
+
+        def store_codes(j, first, last):
+            nc.sync.dma_start(out=out_1[j].rearrange("p m t -> p (m t)").bitcast(I32)[:, first:last],
+                              in_=y_codes[j][:, first:last].bitcast(I32))
+
+        def store_scales(j):
+            for quad in range(4):
+                nc.sync.dma_start(out=out_2[j, 4 * quad:4 * quad + 4, :].bitcast(I32),
+                                  in_=y_scales[j][32 * quad:32 * quad + 4, :].bitcast(I32))
+
+        sort_x_codes(0, 0, 2)
+        sort_x_scales(0, 0, 2)
+        sort_x_scales(0, 2, 4)
+        sort_x_codes(0, 2, 4)
+        nc.vector.tensor_copy(out=decay_f[:], in_=decay_bf[:])
+        sort_x_scales(1, 0, 4)
+        sort_x_codes(1, 0, 2)
+        h_passes(0, 0, 2)
+        h_passes(1, 0, 2)
+        h_passes(0, 2, 4)
+        h_passes(1, 2, 4)
+        h_passes(2, 0, 4)
+        h_passes(3, 0, 4)
+        for n in range(5):
+            decay_state(n)
+        form_s(0)
+        sort_x_codes(1, 2, 4)
+        form_s(1)
+        h_passes(4, 0, 4)
+        h_passes(5, 0, 4)
+        form_s(2)
+        decay_state(5)
+        form_s(3)
+        decay_state(6)
+        decay_state(7)
+        h_passes(6, 0, 4)
+        turn_q(0)
+        turn_q(1)
+        h_passes(7, 0, 4)
+        form_s(4)
+        mix_s(0, 0, nc.vector.tensor_copy, 0, 128)
+        form_s(5)
+        quantize_s(0, 0)
+        copy_q(0)
+        copy_q(1)
+        decay_state(8)
+        decay_state(9)
+        h_passes(8, 0, 4)
+        h_passes(9, 0, 4)
+        form_s(6)
+        form_s(7)
+        quantize_q(0)
+        silu_gate(0)
+        silu_gate(1)
+        decay_state(10)
+        decay_state(11)
+        mix_s(0, 1, nc.vector.tensor_copy, 0, 128)
+        form_s(8)
+        quantize_s(0, 1)
+        turn_q(2)
+        turn_q(3)
+        copy_q(2)
+        copy_q(3)
+        form_s(9)
+        h_passes(10, 0, 4)
+        o_passes(0)
+
+        last = OUT_UNITS - 1
+        for m in range(OUT_UNITS + 1):
+            n = m + LEAD
+            if m in (1, 3):
+                turn_q(m + 3)
+                turn_q(m + 4)
+                copy_q(m + 3)
+                copy_q(m + 4)
+            if n + 1 < STATE_UNITS:
+                h_passes(n + 1, 0, TOKEN_PASSES)
+            if m % 2 == 1 and m >= 5:
+                turn_y(m - 5, 2)
+            if m <= last:
+                add_local(m)
+            if n % 8 == 0 and n <= STATE_UNITS:
+                mix_s(n // 8 - 1, 1, nc.vector.tensor_copy, 0, 128)
+            if n < STATE_UNITS:
+                form_s(n)
+            if m >= 1:
+                apply_gate(m - 1)
+            if n % 8 == 0 and n <= STATE_UNITS:
+                quantize_s(n // 8 - 1, 1)
+            if n % 8 == 7 and n < STATE_UNITS:
+                quantize_s(n // 8, 0)
+            if m % 2 == 0 and m >= 6:
+                quantize_y(m - 6, 2)
+            if m in (0, 2, 4):
+                quantize_q(m // 2 + 1)
+            if m + 1 <= last:
+                o_passes(m + 1)
+            if m % 2 == 1 and m >= 5:
+                copy_y(m - 5, 2)
+            if n + 2 < STATE_UNITS:
+                decay_state(n + 2)
+            if m + SILU_AHEAD <= last:
+                silu_gate(m + SILU_AHEAD)
+            if n % 8 in (4, 5) and n < STATE_UNITS:
+                mix_s(n // 8, 0, nc.scalar.copy, 64 * (n % 2), 64 * (n % 2 + 1))
+            if m >= 1:
+                round_y(m - 1, nc.scalar.copy)
+            if m % 2 == 0 and 2 <= m < last:
+                store_y(m - 2, 2)
+            if m >= last:
+                store_y(m - 1, 1)
+            if m % 4 == 0 and m >= 8:
+                half = (m - 8) // 4
+                store_codes(half // 2, KP * (half % 2), KP * (half % 2 + 1))
+                if half % 2 == 1:
+                    store_scales(half // 2)
+            if m == last:
+                turn_y(last - 3, 2)
+                copy_y(last - 3, 2)
+                turn_y(last - 1, 1)
+                copy_y(last - 1, 1)
+        quantize_y(last - 3, 2)
+        quantize_y(last - 1, 1)
+        turn_y(last, 1)
+        copy_y(last, 1)
+        quantize_y(last, 1)
+        store_codes(CHUNKS - 1, KP, R)
+        store_scales(CHUNKS - 1)

@@ -26,7 +26,7 @@ ROW_TILES = R // P
 STATE_UNITS = CHUNKS * KEY_PASSES * PACK
 OUT_UNITS = CHUNKS * ROW_TILES
 LEAD = 10
-SILU_AHEAD = 2
+SILU_AHEAD = 4
 
 
 def tile_decayed_state_read_h2_kernel(tc, x_words, x_scales, v_words, v_scales, state, decay, queries,
@@ -43,15 +43,18 @@ def tile_decayed_state_read_h2_kernel(tc, x_words, x_scales, v_words, v_scales, 
             return work.tile([P, width], dtype, name=name, tag="big", bufs=4, align_bytes=64)
 
         def interleaved(name, dtype):
-            width = 4096 if dtype == U8 else 2048
-            return work.tile([P, width], dtype, name=name, tag="interleaved", bufs=2, align_bytes=64)
+            return work.tile([P, 2048], dtype, name=name, tag="interleaved", bufs=2, align_bytes=64)
 
         warm = keep.tile([P, 8], F32, name="warm")
         nc.vector.memset(warm[:], 0.0)
-        xs_raw = interleaved("xs_raw", U8)
-        nc.vector.memset(xs_raw[:].bitcast(I32), 0)
-        vs = keep.tile([P, TOKEN_PASSES * E], U8, name="vs", align_bytes=64)
-        nc.vector.memset(vs[:].bitcast(I32), 0)
+        xs_raw, vs = {}, {}
+
+        for part, v_width in enumerate((KP, E - KP)):
+            xs_raw[part] = work.tile([P, TOKEN_PASSES * KP], U8, name="xs_raw%d" % part, tag="y_mixed", bufs=3,
+                                     align_bytes=64)
+            nc.vector.memset(xs_raw[part][:].bitcast(I32), 0)
+            vs[part] = keep.tile([P, TOKEN_PASSES * v_width], U8, name="vs%d" % part, align_bytes=64)
+            nc.vector.memset(vs[part][:].bitcast(I32), 0)
         warm_out = keep.tile([P, 8], F32, name="warm_out")
         nc.scalar.activation(out=warm_out[:], in_=warm[:], func=ACT.Silu)
 
@@ -65,9 +68,9 @@ def tile_decayed_state_read_h2_kernel(tc, x_words, x_scales, v_words, v_scales, 
             nc.sync.dma_start(out=x_raw[g][:, KP * c0:KP * c1].rearrange("p (c n) -> p c n", n=KP),
                               in_=x_by_partition[:, c0:c1, 4 * KP * g:4 * KP * (g + 1)].bitcast(I32))
 
-        def load_scales(queue, plane, scales, quads):
+        def load_scales(plane, scales, quads):
             for quad in quads:
-                queue.dma_start(
+                nc.sync.dma_start(
                     out=plane[32 * quad:32 * quad + 4, :].bitcast(I32).rearrange("p (c n) -> p c n", c=TOKEN_PASSES),
                     in_=scales[:, 4 * quad:4 * quad + 4, :].rearrange("c r n -> r c n").bitcast(I32))
 
@@ -82,10 +85,11 @@ def tile_decayed_state_read_h2_kernel(tc, x_words, x_scales, v_words, v_scales, 
                 out=state_sb[j, g][:].rearrange("p (t e) -> p t e", t=PACK),
                 in_=state[KP * g:KP * (g + 1), KP * j:KP * (j + 1)].rearrange("(p t) e -> p t e", t=PACK))
 
-        def load_q(h):
-            q_sb[h] = big("q%d" % h, BF16)
-            nc.sync.dma_start(out=q_sb[h][:].rearrange("p (i d) -> p i d", i=4),
-                              in_=queries[KP * h:KP * (h + 1), :].rearrange("(i p) d -> p i d", p=P))
+        def load_q(a):
+            if a % 2 == 0:
+                q_sb[a // 2] = big("q%d" % (a // 2), BF16)
+            nc.sync.dma_start(out=q_sb[a // 2][:, 2 * D * (a % 2):2 * D * (a % 2 + 1)].rearrange("p (i d) -> p i d", i=2),
+                              in_=queries[2 * P * a:2 * P * (a + 1), :].rearrange("(i p) d -> p i d", p=P))
 
         def load_rows(store, source, label, j, h):
             store[j, h] = keep.tile([P, 4 * KP], BF16, name="%s%d%d" % (label, j, h))
@@ -97,28 +101,33 @@ def tile_decayed_state_read_h2_kernel(tc, x_words, x_scales, v_words, v_scales, 
             load_rows(gate_sb, gate, "gate", j, h)
             load_rows(local_sb, local_part, "local", j, h)
 
-        load_scales(nc.gpsimd, vs, v_scales, (0, 1))
-        decay_bf = keep.tile([P, KEY_PASSES * PACK], BF16, name="decay_bf")
-        nc.gpsimd.dma_start(out=decay_bf[:].rearrange("p (g t) -> p g t", t=PACK),
-                            in_=decay.rearrange("(g p t) -> p g t", p=P, t=PACK))
         ident = keep.tile([P, P], F32, name="ident")
-        make_identity(nc, ident[:])
+        nc.vector.memset(ident[:], 0.0)
+        make_identity(nc, ident[:], nomemset=True)
 
+        load_scales(xs_raw[0], x_scales[:, :, :KP], range(4))
         load_x(0, 0, 2)
         load_v(0)
-        load_scales(nc.sync, xs_raw, x_scales, range(4))
-        load_scales(nc.sync, vs, v_scales, (2, 3))
+        load_scales(vs[0], v_scales[:, :, :KP], range(4))
         load_x(0, 2, 4)
+        decay_bf = keep.tile([P, KEY_PASSES * PACK], BF16, name="decay_bf")
+        nc.sync.dma_start(out=decay_bf[:].rearrange("p (g t) -> p g t", t=PACK),
+                          in_=decay.rearrange("(g p t) -> p g t", p=P, t=PACK))
         load_x(1, 0, 2)
+        load_scales(xs_raw[1], x_scales[:, :, KP:], range(4))
         load_state(0, 0)
         load_x(1, 2, 4)
         load_state(0, 1)
+        load_rows(gate_sb, gate, "gate", 0, 0)
         load_q(0)
         load_v(1)
+        load_scales(vs[1], v_scales[:, :, KP:], range(4))
         load_state(1, 0)
-        load_gate_local(0, 0)
+        load_rows(local_sb, local_part, "local", 0, 0)
         load_q(1)
         load_gate_local(0, 1)
+        load_q(2)
+        load_q(3)
         load_state(1, 1)
         load_v(2)
         load_state(2, 0)
@@ -133,10 +142,9 @@ def tile_decayed_state_read_h2_kernel(tc, x_words, x_scales, v_words, v_scales, 
         def sort_x_scales(g, c0, c1):
             if g not in x_sc:
                 x_sc[g] = keep.tile([P, TOKEN_PASSES * KP], U8, name="x_sc%d" % g, align_bytes=64)
-            src = xs_raw[:].rearrange("p (c n) -> p c n", c=TOKEN_PASSES)[:, c0:c1, KP * g:KP * (g + 1)]
             nc.vector.tensor_copy(
                 out=x_sc[g][:, KP * c0:KP * c1].rearrange("p (c t a i) -> p c a t i", t=PACK, a=8, i=16),
-                in_=src.rearrange("p c (a i t) -> p c a t i", t=PACK, i=16))
+                in_=xs_raw[g][:, KP * c0:KP * c1].rearrange("p (c a i t) -> p c a t i", t=PACK, a=8, i=16))
 
         def sort_x_codes(g, c0, c1):
             if g not in x_codes:
@@ -153,6 +161,12 @@ def tile_decayed_state_read_h2_kernel(tc, x_words, x_scales, v_words, v_scales, 
         def unit(n):
             return n // 8, n // 4 % 2, n % 4
 
+        def v_plane(j, c):
+            if j == 0:
+                return vs[0][:, KP * c:KP * (c + 1)]
+            first = (E - KP) * c + KP * (j - 1)
+            return vs[1][:, first:first + KP]
+
         def h_passes(n, c0, c1):
             j, g, t = unit(n)
             if c0 == 0:
@@ -162,7 +176,7 @@ def tile_decayed_state_read_h2_kernel(tc, x_words, x_scales, v_words, v_scales, 
                 nc.tensor.matmul_mx(
                     out=h_bank[n][:], lhsT=x_codes[g][:, cols].bitcast(FP8X4), lhsT_scale=x_sc[g][:, cols],
                     rhs=v_codes[j][:, 2 * KP * c:2 * KP * (c + 1)].bitcast(FP4X4),
-                    rhs_scale=vs[:, E * c + KP * j:E * c + KP * (j + 1)],
+                    rhs_scale=v_plane(j, c),
                     start=(c == 0), stop=(c == TOKEN_PASSES - 1))
 
         def decay_state(n):
@@ -242,16 +256,19 @@ def tile_decayed_state_read_h2_kernel(tc, x_words, x_scales, v_words, v_scales, 
         def y_rows(m):
             return y_sb[m // 4][:, KP * (m % 4):KP * (m % 4 + 1)]
 
-        def apply_gate(m):
+        def apply_gate(m, engine):
             if m % 4 == 0:
                 y_sb[m // 4] = big("y%d" % (m // 4), F32)
-            nc.vector.tensor_tensor(out=y_rows(m), in0=summed[m][:], in1=silu[m][:], op=ALU.mult)
+            engine.tensor_tensor(out=y_rows(m), in0=summed[m][:], in1=silu[m][:], op=ALU.mult)
 
         def store_y(m0, count):
             j, i = divmod(m0, ROW_TILES)
             nc.sync.dma_start(
                 out=out_0[P * i:P * (i + count), KP * j:KP * (j + 1)].rearrange("(i p) e -> p i e", p=P),
                 in_=y_sb[m0 // 4][:, KP * (m0 % 4):KP * (m0 % 4 + count)].rearrange("p (i e) -> p i e", e=KP))
+
+        def pool_copy(out, in_):
+            nc.gpsimd.tensor_scalar(out=out, in0=in_, scalar1=1.0, scalar2=1.0, op0=ALU.mult, op1=ALU.mult)
 
         def round_y(m, copy):
             y_bf[m] = work.tile([P, KP], BF16, name="y_bf%d" % m, tag="y_bf", bufs=4)
@@ -266,10 +283,10 @@ def tile_decayed_state_read_h2_kernel(tc, x_words, x_scales, v_words, v_scales, 
                     nc.tensor.transpose(y_bank[m0][:, P * (2 * b + u):P * (2 * b + u + 1)],
                                         words[:, P * u:P * (u + 1)], ident[:])
 
-        def copy_y(m0, count):
+        def copy_y(m0, count, copy):
             y_mixed[m0] = work.tile([P, KP * count], BF16, name="y_mixed%d" % m0, tag="y_mixed", bufs=3, align_bytes=64)
-            nc.scalar.copy(out=y_mixed[m0][:].bitcast(F32).rearrange("p (b r u) -> p b r u", b=count, u=2),
-                           in_=y_bank[m0][:, :2 * P * count].rearrange("p (b u r) -> p b r u", b=count, u=2))
+            copy(out=y_mixed[m0][:].bitcast(F32).rearrange("p (b r u) -> p b r u", b=count, u=2),
+                 in_=y_bank[m0][:, :2 * P * count].rearrange("p (b u r) -> p b r u", b=count, u=2))
 
         def quantize_y(m0, count):
             j, i = divmod(m0, ROW_TILES)
@@ -284,18 +301,18 @@ def tile_decayed_state_read_h2_kernel(tc, x_words, x_scales, v_words, v_scales, 
             nc.sync.dma_start(out=out_1[j].rearrange("p m t -> p (m t)").bitcast(I32)[:, first:last],
                               in_=y_codes[j][:, first:last].bitcast(I32))
 
-        def store_scales(j):
+        def store_scales(j, queues):
             for quad in range(4):
-                nc.sync.dma_start(out=out_2[j, 4 * quad:4 * quad + 4, :].bitcast(I32),
+                queues[quad % len(queues)].dma_start(out=out_2[j, 4 * quad:4 * quad + 4, :].bitcast(I32),
                                   in_=y_scales[j][32 * quad:32 * quad + 4, :].bitcast(I32))
 
-        sort_x_codes(0, 0, 2)
         sort_x_scales(0, 0, 2)
+        sort_x_codes(0, 0, 2)
         sort_x_scales(0, 2, 4)
         sort_x_codes(0, 2, 4)
         nc.vector.tensor_copy(out=decay_f[:], in_=decay_bf[:])
-        sort_x_scales(1, 0, 4)
         sort_x_codes(1, 0, 2)
+        sort_x_scales(1, 0, 4)
         h_passes(0, 0, 2)
         h_passes(1, 0, 2)
         h_passes(0, 2, 4)
@@ -307,55 +324,49 @@ def tile_decayed_state_read_h2_kernel(tc, x_words, x_scales, v_words, v_scales, 
         form_s(0)
         sort_x_codes(1, 2, 4)
         form_s(1)
-        h_passes(4, 0, 4)
-        h_passes(5, 0, 4)
-        form_s(2)
-        decay_state(5)
-        form_s(3)
-        decay_state(6)
-        decay_state(7)
-        h_passes(6, 0, 4)
+        for n in range(4, 8):
+            if n < 7:
+                decay_state(n + 1)
+            form_s(n - 2)
+            h_passes(n, 0, 4)
+            if n == 6:
+                mix_s(0, 0, nc.vector.tensor_copy, 0, 128)
+        quantize_s(0, 0)
         turn_q(0)
         turn_q(1)
-        h_passes(7, 0, 4)
-        form_s(4)
-        mix_s(0, 0, nc.vector.tensor_copy, 0, 128)
-        form_s(5)
-        quantize_s(0, 0)
-        copy_q(0)
-        copy_q(1)
-        decay_state(8)
-        decay_state(9)
         h_passes(8, 0, 4)
         h_passes(9, 0, 4)
         form_s(6)
         form_s(7)
-        quantize_q(0)
-        silu_gate(0)
-        silu_gate(1)
-        decay_state(10)
-        decay_state(11)
+        for m in range(SILU_AHEAD):
+            silu_gate(m)
+        copy_q(0)
+        copy_q(1)
+        for n in range(8, 12):
+            decay_state(n)
         mix_s(0, 1, nc.vector.tensor_copy, 0, 128)
-        form_s(8)
+        quantize_q(0)
         quantize_s(0, 1)
+        form_s(8)
+        o_passes(0)
+        form_s(9)
+        h_passes(10, 0, 4)
         turn_q(2)
         turn_q(3)
         copy_q(2)
         copy_q(3)
-        form_s(9)
-        h_passes(10, 0, 4)
-        o_passes(0)
 
         last = OUT_UNITS - 1
         for m in range(OUT_UNITS + 1):
             n = m + LEAD
+            opens_chunk = (m + 1) % ROW_TILES == 0
+            if m < last and not opens_chunk and m not in (1, 3, 5):
+                o_passes(m + 1)
             if m in (1, 3):
                 turn_q(m + 3)
                 turn_q(m + 4)
                 copy_q(m + 3)
                 copy_q(m + 4)
-            if n + 1 < STATE_UNITS:
-                h_passes(n + 1, 0, TOKEN_PASSES)
             if m % 2 == 1 and m >= 5:
                 turn_y(m - 5, 2)
             if m <= last:
@@ -365,26 +376,30 @@ def tile_decayed_state_read_h2_kernel(tc, x_words, x_scales, v_words, v_scales, 
             if n < STATE_UNITS:
                 form_s(n)
             if m >= 1:
-                apply_gate(m - 1)
+                apply_gate(m - 1, nc.vector)
+            if m in (1, 2, 4):
+                quantize_q(m // 2 + 1)
             if n % 8 == 0 and n <= STATE_UNITS:
                 quantize_s(n // 8 - 1, 1)
             if n % 8 == 7 and n < STATE_UNITS:
                 quantize_s(n // 8, 0)
             if m % 2 == 0 and m >= 6:
                 quantize_y(m - 6, 2)
-            if m in (0, 2, 4):
-                quantize_q(m // 2 + 1)
-            if m + 1 <= last:
+            if m in (1, 3, 5):
+                o_passes(m + 1)
+            if n + 1 < STATE_UNITS:
+                h_passes(n + 1, 0, TOKEN_PASSES)
+            if m < last and opens_chunk:
                 o_passes(m + 1)
             if m % 2 == 1 and m >= 5:
-                copy_y(m - 5, 2)
+                copy_y(m - 5, 2, nc.scalar.copy)
             if n + 2 < STATE_UNITS:
                 decay_state(n + 2)
             if m + SILU_AHEAD <= last:
                 silu_gate(m + SILU_AHEAD)
             if n % 8 in (4, 5) and n < STATE_UNITS:
                 mix_s(n // 8, 0, nc.scalar.copy, 64 * (n % 2), 64 * (n % 2 + 1))
-            if m >= 1:
+            if 1 <= m <= last:
                 round_y(m - 1, nc.scalar.copy)
             if m % 2 == 0 and 2 <= m < last:
                 store_y(m - 2, 2)
@@ -394,16 +409,18 @@ def tile_decayed_state_read_h2_kernel(tc, x_words, x_scales, v_words, v_scales, 
                 half = (m - 8) // 4
                 store_codes(half // 2, KP * (half % 2), KP * (half % 2 + 1))
                 if half % 2 == 1:
-                    store_scales(half // 2)
+                    store_scales(half // 2, [nc.sync])
             if m == last:
                 turn_y(last - 3, 2)
-                copy_y(last - 3, 2)
+                copy_y(last - 3, 2, nc.scalar.copy)
                 turn_y(last - 1, 1)
-                copy_y(last - 1, 1)
+                copy_y(last - 1, 1, nc.scalar.copy)
+        round_y(last, nc.vector.tensor_copy)
         quantize_y(last - 3, 2)
-        quantize_y(last - 1, 1)
         turn_y(last, 1)
-        copy_y(last, 1)
+        quantize_y(last - 1, 1)
+        store_codes(CHUNKS - 1, KP, R - P)
+        copy_y(last, 1, nc.vector.tensor_copy)
         quantize_y(last, 1)
-        store_codes(CHUNKS - 1, KP, R)
-        store_scales(CHUNKS - 1)
+        store_codes(CHUNKS - 1, R - P, R)
+        store_scales(CHUNKS - 1, [nc.scalar, nc.sync])

@@ -97,8 +97,10 @@ def tile_decayed_state_read_h2_kernel(tc, x_words, x_scales, v_words, v_scales, 
                 out=store[j, h][:].rearrange("p (i e) -> p i e", i=4),
                 in_=source[KP * h:KP * (h + 1), KP * j:KP * (j + 1)].rearrange("(i p) e -> p i e", p=P))
 
-        def load_gate_local(j, h):
+        def load_gate(j, h):
             load_rows(gate_sb, gate, "gate", j, h)
+
+        def load_local(j, h):
             load_rows(local_sb, local_part, "local", j, h)
 
         ident = keep.tile([P, P], F32, name="ident")
@@ -113,29 +115,33 @@ def tile_decayed_state_read_h2_kernel(tc, x_words, x_scales, v_words, v_scales, 
         decay_bf = keep.tile([P, KEY_PASSES * PACK], BF16, name="decay_bf")
         nc.sync.dma_start(out=decay_bf[:].rearrange("p (g t) -> p g t", t=PACK),
                           in_=decay.rearrange("(g p t) -> p g t", p=P, t=PACK))
+        load_state(0, 0)
         load_x(1, 0, 2)
         load_scales(xs_raw[1], x_scales[:, :, KP:], range(4))
-        load_state(0, 0)
         load_x(1, 2, 4)
         load_state(0, 1)
-        load_rows(gate_sb, gate, "gate", 0, 0)
         load_q(0)
         load_v(1)
         load_scales(vs[1], v_scales[:, :, KP:], range(4))
-        load_state(1, 0)
-        load_rows(local_sb, local_part, "local", 0, 0)
         load_q(1)
-        load_gate_local(0, 1)
+        load_gate(0, 0)
+        load_local(0, 0)
+        load_state(1, 0)
         load_q(2)
         load_q(3)
+        load_gate(0, 1)
+        load_local(0, 1)
         load_state(1, 1)
+        load_gate(1, 0)
         load_v(2)
         load_state(2, 0)
-        load_gate_local(1, 0)
+        load_local(1, 0)
+        load_gate(1, 1)
         load_state(2, 1)
-        load_gate_local(1, 1)
-        load_gate_local(2, 0)
-        load_gate_local(2, 1)
+        load_local(1, 1)
+        for h in range(2):
+            load_gate(2, h)
+            load_local(2, h)
 
         x_codes, x_sc = {}, {}
 
@@ -193,11 +199,10 @@ def tile_decayed_state_read_h2_kernel(tc, x_words, x_scales, v_words, v_scales, 
                 out=s_rows[j, g][:, KP * t:KP * (t + 1)], in0=h_bank[n][:],
                 scalar=decay_f[:, PACK * g + t:PACK * g + t + 1], in1=decayed[n][:], op0=ALU.mult, op1=ALU.add)
 
-        def mix_s(j, g, copy, a0, a1):
-            if a0 == 0:
-                s_mixed[j, g] = interleaved("s_mixed%d%d" % (j, g), BF16)
-            copy(out=s_mixed[j, g][:].rearrange("p (a i t) -> p a t i", i=4, t=PACK)[:, a0:a1],
-                 in_=s_rows[j, g][:].rearrange("p (t a i) -> p a t i", i=4, t=PACK)[:, a0:a1])
+        def mix_s(j, g, copy):
+            s_mixed[j, g] = interleaved("s_mixed%d%d" % (j, g), BF16)
+            copy(out=s_mixed[j, g][:].rearrange("p (a i t) -> p a t i", i=4, t=PACK),
+                 in_=s_rows[j, g][:].rearrange("p (t a i) -> p a t i", i=4, t=PACK))
 
         def quantize_s(j, g):
             s_codes[j, g] = work.tile([P, KP], U32, name="s_codes%d%d" % (j, g), tag="s_codes", bufs=4, align_bytes=64)
@@ -311,96 +316,121 @@ def tile_decayed_state_read_h2_kernel(tc, x_words, x_scales, v_words, v_scales, 
         sort_x_scales(0, 2, 4)
         sort_x_codes(0, 2, 4)
         nc.vector.tensor_copy(out=decay_f[:], in_=decay_bf[:])
-        sort_x_codes(1, 0, 2)
-        sort_x_scales(1, 0, 4)
         h_passes(0, 0, 2)
         h_passes(1, 0, 2)
         h_passes(0, 2, 4)
         h_passes(1, 2, 4)
         h_passes(2, 0, 4)
         h_passes(3, 0, 4)
-        for n in range(5):
+        for n in range(4):
             decay_state(n)
         form_s(0)
+        sort_x_codes(1, 0, 2)
+        sort_x_scales(1, 0, 4)
         sort_x_codes(1, 2, 4)
         form_s(1)
+        form_s(2)
+        form_s(3)
         for n in range(4, 8):
-            if n < 7:
-                decay_state(n + 1)
-            form_s(n - 2)
+            decay_state(n)
             h_passes(n, 0, 4)
-            if n == 6:
-                mix_s(0, 0, nc.vector.tensor_copy, 0, 128)
-        quantize_s(0, 0)
+            form_s(n)
+            if n == 4:
+                mix_s(0, 0, nc.vector.tensor_copy)
+            if n == 5:
+                quantize_s(0, 0)
         turn_q(0)
         turn_q(1)
         h_passes(8, 0, 4)
-        h_passes(9, 0, 4)
-        form_s(6)
-        form_s(7)
-        for m in range(SILU_AHEAD):
-            silu_gate(m)
         copy_q(0)
         copy_q(1)
-        for n in range(8, 12):
-            decay_state(n)
-        mix_s(0, 1, nc.vector.tensor_copy, 0, 128)
-        quantize_q(0)
-        quantize_s(0, 1)
-        form_s(8)
-        o_passes(0)
-        form_s(9)
-        h_passes(10, 0, 4)
         turn_q(2)
         turn_q(3)
+        mix_s(0, 1, nc.vector.tensor_copy)
+        quantize_q(0)
+        quantize_s(0, 1)
+        o_passes(0)
+        silu_gate(0)
         copy_q(2)
         copy_q(3)
+        decay_state(8)
+        silu_gate(1)
+        decay_state(9)
+        silu_gate(2)
+        silu_gate(3)
 
         last = OUT_UNITS - 1
+
+        def state_unit(m):
+            if m < 2:
+                return 8 + m
+            if m == 2 or m > 12:
+                return None
+            return m + 7 if m < 8 else m + 11
+
         for m in range(OUT_UNITS + 1):
-            n = m + LEAD
-            opens_chunk = (m + 1) % ROW_TILES == 0
-            if m < last and not opens_chunk and m not in (1, 3, 5):
-                o_passes(m + 1)
-            if m in (1, 3):
-                turn_q(m + 3)
-                turn_q(m + 4)
-                copy_q(m + 3)
-                copy_q(m + 4)
-            if m % 2 == 1 and m >= 5:
-                turn_y(m - 5, 2)
-            if m <= last:
-                add_local(m)
-            if n % 8 == 0 and n <= STATE_UNITS:
-                mix_s(n // 8 - 1, 1, nc.vector.tensor_copy, 0, 128)
-            if n < STATE_UNITS:
-                form_s(n)
-            if m >= 1:
+            n = state_unit(m)
+            if m == ROW_TILES:
+                form_s(15)
+                h_passes(16, 0, TOKEN_PASSES)
+                h_passes(17, 0, TOKEN_PASSES)
                 apply_gate(m - 1, nc.vector)
+                mix_s(1, 1, nc.vector.tensor_copy)
+                form_s(16)
+                h_passes(18, 0, TOKEN_PASSES)
+                decay_state(19)
+                quantize_s(1, 1)
+                o_passes(m)
+                form_s(17)
+                h_passes(19, 0, TOKEN_PASSES)
+                form_s(18)
+                decay_state(20)
+            if m <= last and m != 2 * ROW_TILES:
+                add_local(m)
+            if m >= 1 and m != ROW_TILES:
+                apply_gate(m - 1, nc.vector)
+            if m == 2 * ROW_TILES:
+                add_local(m)
             if m in (1, 2, 4):
                 quantize_q(m // 2 + 1)
-            if n % 8 == 0 and n <= STATE_UNITS:
-                quantize_s(n // 8 - 1, 1)
-            if n % 8 == 7 and n < STATE_UNITS:
-                quantize_s(n // 8, 0)
+            if m in (7, 11):
+                quantize_s(m // 4, 0)
+            if m == 15:
+                quantize_s(2, 1)
             if m % 2 == 0 and m >= 6:
                 quantize_y(m - 6, 2)
-            if m in (1, 3, 5):
+            if n is not None:
+                form_s(n)
+            if m < last and m + 1 != ROW_TILES:
                 o_passes(m + 1)
-            if n + 1 < STATE_UNITS:
-                h_passes(n + 1, 0, TOKEN_PASSES)
-            if m < last and opens_chunk:
-                o_passes(m + 1)
-            if m % 2 == 1 and m >= 5:
-                copy_y(m - 5, 2, nc.scalar.copy)
-            if n + 2 < STATE_UNITS:
-                decay_state(n + 2)
+            after = 15 if m == 7 else state_unit(m + 1) if m != 1 else None
+            if after is not None:
+                h_passes(after, 0, TOKEN_PASSES)
+            if m in (0, 2):
+                turn_q(m + 4)
+                turn_q(m + 5)
+            if m % 2 == 0 and m >= 4 and m < last:
+                turn_y(m - 4, 2)
+            if m == 0 or 2 <= m <= 6:
+                decay_state(10 if m == 0 else m + 9)
+            if m == 7:
+                for ahead in range(16, 19):
+                    decay_state(ahead)
+            if 8 <= m <= 10:
+                decay_state(m + 13)
+            if m in (5, 9):
+                mix_s(m // 4, 0, nc.scalar.copy)
+            if m in (0, 2):
+                copy_q(m + 4)
+                copy_q(m + 5)
             if m + SILU_AHEAD <= last:
                 silu_gate(m + SILU_AHEAD)
-            if n % 8 in (4, 5) and n < STATE_UNITS:
-                mix_s(n // 8, 0, nc.scalar.copy, 64 * (n % 2), 64 * (n % 2 + 1))
             if 1 <= m <= last:
-                round_y(m - 1, nc.scalar.copy)
+                round_y(m - 1, pool_copy if m <= 12 else nc.scalar.copy)
+            if m % 2 == 0 and m >= 4 and m < last:
+                copy_y(m - 4, 2, nc.scalar.copy)
+            if m == 12:
+                mix_s(2, 1, nc.scalar.copy)
             if m % 2 == 0 and 2 <= m < last:
                 store_y(m - 2, 2)
             if m >= last:

@@ -49,11 +49,12 @@ def tile_decayed_state_read_h2_kernel(tc, x_words, x_scales, v_words, v_scales, 
         nc.vector.memset(warm[:], 0.0)
         xs_raw, vs = {}, {}
 
-        for part, v_width in enumerate((KP, E - KP)):
-            xs_raw[part] = work.tile([P, TOKEN_PASSES * KP], U8, name="xs_raw%d" % part, tag="y_mixed", bufs=3,
-                                     align_bytes=64)
-            nc.vector.memset(xs_raw[part][:].bitcast(I32), 0)
-            vs[part] = keep.tile([P, TOKEN_PASSES * v_width], U8, name="vs%d" % part, align_bytes=64)
+        for part in range(CHUNKS):
+            if part < KEY_PASSES:
+                xs_raw[part] = work.tile([P, TOKEN_PASSES * KP], U8, name="xs_raw%d" % part, tag="y_mixed", bufs=3,
+                                         align_bytes=64)
+                nc.vector.memset(xs_raw[part][:].bitcast(I32), 0)
+            vs[part] = keep.tile([P, TOKEN_PASSES * KP], U8, name="vs%d" % part, align_bytes=64)
             nc.vector.memset(vs[part][:].bitcast(I32), 0)
         warm_out = keep.tile([P, 8], F32, name="warm_out")
         nc.scalar.activation(out=warm_out[:], in_=warm[:], func=ACT.Silu)
@@ -68,11 +69,12 @@ def tile_decayed_state_read_h2_kernel(tc, x_words, x_scales, v_words, v_scales, 
             nc.sync.dma_start(out=x_raw[g][:, KP * c0:KP * c1].rearrange("p (c n) -> p c n", n=KP),
                               in_=x_by_partition[:, c0:c1, 4 * KP * g:4 * KP * (g + 1)].bitcast(I32))
 
-        def load_scales(plane, scales, quads):
-            for quad in quads:
+        def load_scales(plane, all_scales, part):
+            scales = all_scales[:, :, KP * part:KP * (part + 1)]
+            for row in range(4):
                 nc.sync.dma_start(
-                    out=plane[32 * quad:32 * quad + 4, :].bitcast(I32).rearrange("p (c n) -> p c n", c=TOKEN_PASSES),
-                    in_=scales[:, 4 * quad:4 * quad + 4, :].rearrange("c r n -> r c n").bitcast(I32))
+                    out=plane[row:P:32, :].bitcast(I32).rearrange("p (c n) -> p c n", c=TOKEN_PASSES),
+                    in_=scales[:, row:16:4, :].rearrange("c q n -> q c n").bitcast(I32))
 
         def load_v(j):
             v_codes[j] = keep.tile([P, TOKEN_PASSES * 2 * KP], U8, name="v_codes%d" % j, align_bytes=64)
@@ -91,57 +93,62 @@ def tile_decayed_state_read_h2_kernel(tc, x_words, x_scales, v_words, v_scales, 
             nc.sync.dma_start(out=q_sb[a // 2][:, 2 * D * (a % 2):2 * D * (a % 2 + 1)].rearrange("p (i d) -> p i d", i=2),
                               in_=queries[2 * P * a:2 * P * (a + 1), :].rearrange("(i p) d -> p i d", p=P))
 
-        def load_rows(store, source, label, j, h):
-            store[j, h] = keep.tile([P, 4 * KP], BF16, name="%s%d%d" % (label, j, h))
+        def load_rows(store, source, label, j, first, count):
+            h, i = divmod(first, 4)
+            if i == 0:
+                store[j, h] = keep.tile([P, 4 * KP], BF16, name="%s%d%d" % (label, j, h))
             nc.sync.dma_start(
-                out=store[j, h][:].rearrange("p (i e) -> p i e", i=4),
-                in_=source[KP * h:KP * (h + 1), KP * j:KP * (j + 1)].rearrange("(i p) e -> p i e", p=P))
+                out=store[j, h][:, KP * i:KP * (i + count)].rearrange("p (i e) -> p i e", e=KP),
+                in_=source[P * first:P * (first + count), KP * j:KP * (j + 1)].rearrange("(i p) e -> p i e", p=P))
 
-        def load_gate(j, h):
-            load_rows(gate_sb, gate, "gate", j, h)
+        def load_gate(j, first, count):
+            load_rows(gate_sb, gate, "gate", j, first, count)
 
-        def load_local(j, h):
-            load_rows(local_sb, local_part, "local", j, h)
+        def load_local(j, first, count):
+            load_rows(local_sb, local_part, "local", j, first, count)
 
         ident = keep.tile([P, P], F32, name="ident")
         nc.vector.memset(ident[:], 0.0)
         make_identity(nc, ident[:], nomemset=True)
 
-        load_scales(xs_raw[0], x_scales[:, :, :KP], range(4))
+        load_scales(xs_raw[0], x_scales, 0)
         load_x(0, 0, 2)
         load_v(0)
-        load_scales(vs[0], v_scales[:, :, :KP], range(4))
+        load_scales(vs[0], v_scales, 0)
         load_x(0, 2, 4)
         decay_bf = keep.tile([P, KEY_PASSES * PACK], BF16, name="decay_bf")
         nc.sync.dma_start(out=decay_bf[:].rearrange("p (g t) -> p g t", t=PACK),
                           in_=decay.rearrange("(g p t) -> p g t", p=P, t=PACK))
-        load_state(0, 0)
+        load_scales(xs_raw[1], x_scales, 1)
         load_x(1, 0, 2)
-        load_scales(xs_raw[1], x_scales[:, :, KP:], range(4))
+        load_state(0, 0)
         load_x(1, 2, 4)
         load_state(0, 1)
         load_q(0)
         load_v(1)
-        load_scales(vs[1], v_scales[:, :, KP:], range(4))
+        load_scales(vs[1], v_scales, 1)
         load_q(1)
-        load_gate(0, 0)
-        load_local(0, 0)
         load_state(1, 0)
+        load_local(0, 0, 2)
+        load_gate(0, 0, 2)
         load_q(2)
+        load_local(0, 2, 2)
+        load_gate(0, 2, 2)
         load_q(3)
-        load_gate(0, 1)
-        load_local(0, 1)
+        load_gate(0, 4, 4)
+        load_local(0, 4, 4)
         load_state(1, 1)
-        load_gate(1, 0)
+        load_gate(1, 0, 4)
         load_v(2)
+        load_scales(vs[2], v_scales, 2)
         load_state(2, 0)
-        load_local(1, 0)
-        load_gate(1, 1)
+        load_local(1, 0, 4)
+        load_gate(1, 4, 4)
         load_state(2, 1)
-        load_local(1, 1)
+        load_local(1, 4, 4)
         for h in range(2):
-            load_gate(2, h)
-            load_local(2, h)
+            load_gate(2, 4 * h, 4)
+            load_local(2, 4 * h, 4)
 
         x_codes, x_sc = {}, {}
 
@@ -167,12 +174,6 @@ def tile_decayed_state_read_h2_kernel(tc, x_words, x_scales, v_words, v_scales, 
         def unit(n):
             return n // 8, n // 4 % 2, n % 4
 
-        def v_plane(j, c):
-            if j == 0:
-                return vs[0][:, KP * c:KP * (c + 1)]
-            first = (E - KP) * c + KP * (j - 1)
-            return vs[1][:, first:first + KP]
-
         def h_passes(n, c0, c1):
             j, g, t = unit(n)
             if c0 == 0:
@@ -182,7 +183,7 @@ def tile_decayed_state_read_h2_kernel(tc, x_words, x_scales, v_words, v_scales, 
                 nc.tensor.matmul_mx(
                     out=h_bank[n][:], lhsT=x_codes[g][:, cols].bitcast(FP8X4), lhsT_scale=x_sc[g][:, cols],
                     rhs=v_codes[j][:, 2 * KP * c:2 * KP * (c + 1)].bitcast(FP4X4),
-                    rhs_scale=v_plane(j, c),
+                    rhs_scale=vs[j][:, KP * c:KP * (c + 1)],
                     start=(c == 0), stop=(c == TOKEN_PASSES - 1))
 
         def decay_state(n):
@@ -199,10 +200,14 @@ def tile_decayed_state_read_h2_kernel(tc, x_words, x_scales, v_words, v_scales, 
                 out=s_rows[j, g][:, KP * t:KP * (t + 1)], in0=h_bank[n][:],
                 scalar=decay_f[:, PACK * g + t:PACK * g + t + 1], in1=decayed[n][:], op0=ALU.mult, op1=ALU.add)
 
-        def mix_s(j, g, copy):
+        def mix_s(j, g, on_vector):
             s_mixed[j, g] = interleaved("s_mixed%d%d" % (j, g), BF16)
-            copy(out=s_mixed[j, g][:].rearrange("p (a i t) -> p a t i", i=4, t=PACK),
-                 in_=s_rows[j, g][:].rearrange("p (t a i) -> p a t i", i=4, t=PACK))
+            out = s_mixed[j, g][:].rearrange("p (a i t) -> p a t i", i=4, t=PACK)
+            in_ = s_rows[j, g][:].rearrange("p (t a i) -> p a t i", i=4, t=PACK)
+            if on_vector > 0:
+                nc.vector.tensor_copy(out=out[:, :on_vector], in_=in_[:, :on_vector])
+            if on_vector < P:
+                nc.scalar.copy(out=out[:, on_vector:], in_=in_[:, on_vector:])
 
         def quantize_s(j, g):
             s_codes[j, g] = work.tile([P, KP], U32, name="s_codes%d%d" % (j, g), tag="s_codes", bufs=4, align_bytes=64)
@@ -307,7 +312,7 @@ def tile_decayed_state_read_h2_kernel(tc, x_words, x_scales, v_words, v_scales, 
                               in_=y_codes[j][:, first:last].bitcast(I32))
 
         def store_scales(j, queues):
-            for quad in range(4):
+            for quad in (0, 2, 1, 3):
                 queues[quad % len(queues)].dma_start(out=out_2[j, 4 * quad:4 * quad + 4, :].bitcast(I32),
                                   in_=y_scales[j][32 * quad:32 * quad + 4, :].bitcast(I32))
 
@@ -324,21 +329,21 @@ def tile_decayed_state_read_h2_kernel(tc, x_words, x_scales, v_words, v_scales, 
         h_passes(3, 0, 4)
         for n in range(4):
             decay_state(n)
-        form_s(0)
-        sort_x_codes(1, 0, 2)
         sort_x_scales(1, 0, 4)
+        sort_x_codes(1, 0, 2)
+        form_s(0)
+        h_passes(4, 0, 2)
+        h_passes(5, 0, 2)
         sort_x_codes(1, 2, 4)
         form_s(1)
         form_s(2)
         form_s(3)
         for n in range(4, 8):
             decay_state(n)
-            h_passes(n, 0, 4)
+            h_passes(n, 2 if n < 6 else 0, 4)
+            if n == 7:
+                mix_s(0, 0, 48)
             form_s(n)
-            if n == 4:
-                mix_s(0, 0, nc.vector.tensor_copy)
-            if n == 5:
-                quantize_s(0, 0)
         turn_q(0)
         turn_q(1)
         h_passes(8, 0, 4)
@@ -346,14 +351,16 @@ def tile_decayed_state_read_h2_kernel(tc, x_words, x_scales, v_words, v_scales, 
         copy_q(1)
         turn_q(2)
         turn_q(3)
-        mix_s(0, 1, nc.vector.tensor_copy)
+        quantize_s(0, 0)
+        mix_s(0, 1, 128)
         quantize_q(0)
         quantize_s(0, 1)
         o_passes(0)
-        silu_gate(0)
+        decay_state(8)
         copy_q(2)
         copy_q(3)
-        decay_state(8)
+        form_s(8)
+        silu_gate(0)
         silu_gate(1)
         decay_state(9)
         silu_gate(2)
@@ -362,9 +369,9 @@ def tile_decayed_state_read_h2_kernel(tc, x_words, x_scales, v_words, v_scales, 
         last = OUT_UNITS - 1
 
         def state_unit(m):
-            if m < 2:
-                return 8 + m
-            if m == 2 or m > 12:
+            if m == 1:
+                return 9
+            if m in (0, 2) or m > 12:
                 return None
             return m + 7 if m < 8 else m + 11
 
@@ -375,7 +382,7 @@ def tile_decayed_state_read_h2_kernel(tc, x_words, x_scales, v_words, v_scales, 
                 h_passes(16, 0, TOKEN_PASSES)
                 h_passes(17, 0, TOKEN_PASSES)
                 apply_gate(m - 1, nc.vector)
-                mix_s(1, 1, nc.vector.tensor_copy)
+                mix_s(1, 1, 128)
                 form_s(16)
                 h_passes(18, 0, TOKEN_PASSES)
                 decay_state(19)
@@ -385,17 +392,17 @@ def tile_decayed_state_read_h2_kernel(tc, x_words, x_scales, v_words, v_scales, 
                 h_passes(19, 0, TOKEN_PASSES)
                 form_s(18)
                 decay_state(20)
-            if m <= last and m != 2 * ROW_TILES:
+            if m <= last:
                 add_local(m)
+            if m == 13:
+                mix_s(2, 1, 40)
             if m >= 1 and m != ROW_TILES:
                 apply_gate(m - 1, nc.vector)
-            if m == 2 * ROW_TILES:
-                add_local(m)
-            if m in (1, 2, 4):
+            if m in (0, 2, 4):
                 quantize_q(m // 2 + 1)
             if m in (7, 11):
                 quantize_s(m // 4, 0)
-            if m == 15:
+            if m == 14:
                 quantize_s(2, 1)
             if m % 2 == 0 and m >= 6:
                 quantize_y(m - 6, 2)
@@ -419,7 +426,7 @@ def tile_decayed_state_read_h2_kernel(tc, x_words, x_scales, v_words, v_scales, 
             if 8 <= m <= 10:
                 decay_state(m + 13)
             if m in (5, 9):
-                mix_s(m // 4, 0, nc.scalar.copy)
+                mix_s(m // 4, 0, 0)
             if m in (0, 2):
                 copy_q(m + 4)
                 copy_q(m + 5)
@@ -429,8 +436,6 @@ def tile_decayed_state_read_h2_kernel(tc, x_words, x_scales, v_words, v_scales, 
                 round_y(m - 1, pool_copy if m <= 12 else nc.scalar.copy)
             if m % 2 == 0 and m >= 4 and m < last:
                 copy_y(m - 4, 2, nc.scalar.copy)
-            if m == 12:
-                mix_s(2, 1, nc.scalar.copy)
             if m % 2 == 0 and 2 <= m < last:
                 store_y(m - 2, 2)
             if m >= last:

from contextlib import ExitStack

import concourse.mybir as mybir
from concourse.masks import make_identity

C, D, E, R = 2048, 1024, 1536, 1024
FLOPS = 2 * C * D * E + 2 * R * D * E

F32 = mybir.dt.float32
BF16 = mybir.dt.bfloat16
I32 = mybir.dt.int32
U32 = mybir.dt.uint32
U8 = mybir.dt.uint8
FP8X4 = mybir.dt.float8_e4m3fn_x4
FP4X4 = mybir.dt.float4_e2m1fn_x4
ACT = mybir.ActivationFunctionType
ALU = mybir.AluOpType

P = 128
PACK = 4
KP = P * PACK
TOKEN_PASSES = C // KP
KEY_PASSES = D // KP
CHUNKS = E // KP
ROW_TILES = R // P
STATE_UNITS = CHUNKS * KEY_PASSES * PACK
OUT_UNITS = CHUNKS * ROW_TILES
LEAD = 10
SILU_AHEAD = 4


def tile_decayed_state_read_h2_kernel(tc, x_words, x_scales, v_words, v_scales, state, decay, queries,
                                                 local_part, gate, out_0, out_1, out_2):
    nc = tc.nc
    with ExitStack() as ctx:
        keep = ctx.enter_context(tc.tile_pool(name="keep", bufs=1))
        work = ctx.enter_context(tc.tile_pool(name="work", bufs=2))
        psum = ctx.enter_context(tc.psum_pool(name="psum", bufs=2))
        ctx.enter_context(tc.manual_schedule())

        def big(name, dtype):
            width = 4096 if dtype == BF16 else 2048
            return work.tile([P, width], dtype, name=name, tag="big", bufs=4, align_bytes=64)

        def interleaved(name, dtype):
            return work.tile([P, 2048], dtype, name=name, tag="interleaved", bufs=2, align_bytes=64)

        warm = keep.tile([P, 8], F32, name="warm")
        nc.vector.memset(warm[:], 0.0)
        xs_raw, vs = {}, {}

        for part in range(CHUNKS):
            if part < KEY_PASSES:
                xs_raw[part] = work.tile([P, TOKEN_PASSES * KP], U8, name="xs_raw%d" % part, tag="y_mixed", bufs=3,
                                         align_bytes=64)
                nc.vector.memset(xs_raw[part][:].bitcast(I32), 0)
            vs[part] = keep.tile([P, TOKEN_PASSES * KP], U8, name="vs%d" % part, align_bytes=64)
            nc.vector.memset(vs[part][:].bitcast(I32), 0)
        warm_out = keep.tile([P, 8], F32, name="warm_out")
        nc.scalar.activation(out=warm_out[:], in_=warm[:], func=ACT.Silu)

        x_by_partition = x_words.rearrange("c p n t -> p c (n t)")
        v_by_partition = v_words.rearrange("c p n -> p c n")
        x_raw, v_codes, state_sb, q_sb, gate_sb, local_sb = {}, {}, {}, {}, {}, {}

        def load_x(g, c0, c1):
            if g not in x_raw:
                x_raw[g] = big("x_raw%d" % g, I32)
            nc.sync.dma_start(out=x_raw[g][:, KP * c0:KP * c1].rearrange("p (c n) -> p c n", n=KP),
                              in_=x_by_partition[:, c0:c1, 4 * KP * g:4 * KP * (g + 1)].bitcast(I32))

        def load_scales(plane, all_scales, part):
            scales = all_scales[:, :, KP * part:KP * (part + 1)]
            for row in range(4):
                nc.sync.dma_start(
                    out=plane[row:P:32, :].bitcast(I32).rearrange("p (c n) -> p c n", c=TOKEN_PASSES),
                    in_=scales[:, row:16:4, :].rearrange("c q n -> q c n").bitcast(I32))

        def load_v(j):
            v_codes[j] = keep.tile([P, TOKEN_PASSES * 2 * KP], U8, name="v_codes%d" % j, align_bytes=64)
            nc.sync.dma_start(out=v_codes[j][:].bitcast(I32).rearrange("p (c n) -> p c n", c=TOKEN_PASSES),
                              in_=v_by_partition[:, :, 2 * KP * j:2 * KP * (j + 1)].bitcast(I32))

        def load_state(j, g):
            state_sb[j, g] = keep.tile([P, PACK * KP], BF16, name="state%d%d" % (j, g))
            nc.sync.dma_start(
                out=state_sb[j, g][:].rearrange("p (t e) -> p t e", t=PACK),
                in_=state[KP * g:KP * (g + 1), KP * j:KP * (j + 1)].rearrange("(p t) e -> p t e", t=PACK))

        def load_q(a):
            if a % 2 == 0:
                q_sb[a // 2] = big("q%d" % (a // 2), BF16)
            nc.sync.dma_start(out=q_sb[a // 2][:, 2 * D * (a % 2):2 * D * (a % 2 + 1)].rearrange("p (i d) -> p i d", i=2),
                              in_=queries[2 * P * a:2 * P * (a + 1), :].rearrange("(i p) d -> p i d", p=P))

        def load_rows(store, source, label, j, first, count):
            h, i = divmod(first, 4)
            if i == 0:
                store[j, h] = keep.tile([P, 4 * KP], BF16, name="%s%d%d" % (label, j, h))
            nc.sync.dma_start(
                out=store[j, h][:, KP * i:KP * (i + count)].rearrange("p (i e) -> p i e", e=KP),
                in_=source[P * first:P * (first + count), KP * j:KP * (j + 1)].rearrange("(i p) e -> p i e", p=P))

        def load_gate(j, first, count):
            load_rows(gate_sb, gate, "gate", j, first, count)

        def load_local(j, first, count):
            load_rows(local_sb, local_part, "local", j, first, count)

        ident = keep.tile([P, P], F32, name="ident")
        nc.vector.memset(ident[:], 0.0)
        make_identity(nc, ident[:], nomemset=True)

        load_scales(xs_raw[0], x_scales, 0)
        load_x(0, 0, 2)
        load_v(0)
        load_scales(vs[0], v_scales, 0)
        load_x(0, 2, 4)
        decay_bf = keep.tile([P, KEY_PASSES * PACK], BF16, name="decay_bf")
        nc.sync.dma_start(out=decay_bf[:].rearrange("p (g t) -> p g t", t=PACK),
                          in_=decay.rearrange("(g p t) -> p g t", p=P, t=PACK))
        load_scales(xs_raw[1], x_scales, 1)
        load_x(1, 0, 2)
        load_state(0, 0)
        load_x(1, 2, 4)
        load_state(0, 1)
        load_q(0)
        load_v(1)
        load_scales(vs[1], v_scales, 1)
        load_q(1)
        load_state(1, 0)
        load_local(0, 0, 2)
        load_gate(0, 0, 2)
        load_q(2)
        load_local(0, 2, 2)
        load_gate(0, 2, 2)
        load_q(3)
        load_gate(0, 4, 4)
        load_local(0, 4, 4)
        load_state(1, 1)
        load_gate(1, 0, 4)
        load_v(2)
        load_scales(vs[2], v_scales, 2)
        load_state(2, 0)
        load_local(1, 0, 4)
        load_gate(1, 4, 4)
        load_state(2, 1)
        load_local(1, 4, 4)
        for h in range(2):
            load_gate(2, 4 * h, 4)
            load_local(2, 4 * h, 4)

        x_codes, x_sc = {}, {}

        def sort_x_scales(g, c0, c1):
            if g not in x_sc:
                x_sc[g] = keep.tile([P, TOKEN_PASSES * KP], U8, name="x_sc%d" % g, align_bytes=64)
            nc.vector.tensor_copy(
                out=x_sc[g][:, KP * c0:KP * c1].rearrange("p (c t a i) -> p c a t i", t=PACK, a=8, i=16),
                in_=xs_raw[g][:, KP * c0:KP * c1].rearrange("p (c a i t) -> p c a t i", t=PACK, a=8, i=16))

        def sort_x_codes(g, c0, c1):
            if g not in x_codes:
                x_codes[g] = keep.tile([P, TOKEN_PASSES * KP], I32, name="x_codes%d" % g, align_bytes=64)
            cols = slice(KP * c0, KP * c1)
            nc.vector.tensor_copy(
                out=x_codes[g][:, cols].rearrange("p (c t a i) -> p c a t i", t=PACK, a=32, i=4),
                in_=x_raw[g][:, cols].rearrange("p (c a i t) -> p c a t i", t=PACK, a=32, i=4))

        decay_f = keep.tile([P, KEY_PASSES * PACK], F32, name="decay_f")

        h_bank, decayed, s_rows, s_mixed, s_codes, s_scales = {}, {}, {}, {}, {}, {}

        def unit(n):
            return n // 8, n // 4 % 2, n % 4

        def h_passes(n, c0, c1):
            j, g, t = unit(n)
            if c0 == 0:
                h_bank[n] = psum.tile([P, KP], F32, name="h%d" % n, tag="acc", bufs=6)
            for c in range(c0, c1):
                cols = slice(KP * c + P * t, KP * c + P * (t + 1))
                nc.tensor.matmul_mx(
                    out=h_bank[n][:], lhsT=x_codes[g][:, cols].bitcast(FP8X4), lhsT_scale=x_sc[g][:, cols],
                    rhs=v_codes[j][:, 2 * KP * c:2 * KP * (c + 1)].bitcast(FP4X4),
                    rhs_scale=vs[j][:, KP * c:KP * (c + 1)],
                    start=(c == 0), stop=(c == TOKEN_PASSES - 1))

        def decay_state(n):
            j, g, t = unit(n)
            decayed[n] = work.tile([P, KP], F32, name="decayed%d" % n, tag="decayed", bufs=5)
            nc.scalar.activation(out=decayed[n][:], in_=state_sb[j, g][:, KP * t:KP * (t + 1)], func=ACT.Copy,
                                 scale=decay_f[:, PACK * g + t:PACK * g + t + 1])

        def form_s(n):
            j, g, t = unit(n)
            if t == 0:
                s_rows[j, g] = work.tile([P, PACK * KP], BF16, name="s_rows%d%d" % (j, g), tag="s_rows", bufs=2)
            nc.vector.scalar_tensor_tensor(
                out=s_rows[j, g][:, KP * t:KP * (t + 1)], in0=h_bank[n][:],
                scalar=decay_f[:, PACK * g + t:PACK * g + t + 1], in1=decayed[n][:], op0=ALU.mult, op1=ALU.add)

        def mix_s(j, g, on_vector):
            s_mixed[j, g] = interleaved("s_mixed%d%d" % (j, g), BF16)
            out = s_mixed[j, g][:].rearrange("p (a i t) -> p a t i", i=4, t=PACK)
            in_ = s_rows[j, g][:].rearrange("p (t a i) -> p a t i", i=4, t=PACK)
            if on_vector > 0:
                nc.vector.tensor_copy(out=out[:, :on_vector], in_=in_[:, :on_vector])
            if on_vector < P:
                nc.scalar.copy(out=out[:, on_vector:], in_=in_[:, on_vector:])

        def quantize_s(j, g):
            s_codes[j, g] = work.tile([P, KP], U32, name="s_codes%d%d" % (j, g), tag="s_codes", bufs=4, align_bytes=64)
            s_scales[j, g] = work.tile([P, KP], U8, name="s_scales%d%d" % (j, g), tag="s_scales", bufs=4,
                                       align_bytes=64)
            nc.vector.quantize_mx(out=s_codes[j, g][:].bitcast(FP8X4), scales=s_scales[j, g][:], in_=s_mixed[j, g][:])

        q_bank, q_mixed, q_codes, q_scales = {}, {}, {}, {}

        def turn_q(i):
            q_bank[i] = psum.tile([P, KP], F32, name="q_bank%d" % i, tag="turn", bufs=2)
            words = q_sb[i // 4][:].bitcast(F32)
            for g in range(KEY_PASSES):
                for u in range(2):
                    first = KP * (i % 4) + 256 * g
                    nc.tensor.transpose(q_bank[i][:, P * (2 * g + u):P * (2 * g + u + 1)],
                                        words[:, first + u:first + 256:2], ident[:])

        def copy_q(i):
            if i % 2 == 0:
                q_mixed[i // 2] = work.tile([P, 2048], BF16, name="q_mixed%d" % (i // 2), tag="q_mixed", bufs=2,
                                            align_bytes=64)
            words = q_mixed[i // 2][:].bitcast(F32)[:, KP * (i % 2):KP * (i % 2 + 1)]
            nc.scalar.copy(out=words.rearrange("p (g r u) -> p g r u", g=KEY_PASSES, u=2),
                           in_=q_bank[i][:].rearrange("p (g u r) -> p g r u", g=KEY_PASSES, u=2))

        def quantize_q(a):
            q_codes[a] = keep.tile([P, KP], U32, name="q_codes%d" % a, align_bytes=64)
            q_scales[a] = keep.tile([P, KP], U8, name="q_scales%d" % a, align_bytes=64)
            nc.vector.quantize_mx(out=q_codes[a][:].bitcast(FP8X4), scales=q_scales[a][:], in_=q_mixed[a][:])

        o_bank, silu, summed, y_sb, y_bf, y_bank, y_mixed, y_codes, y_scales = {}, {}, {}, {}, {}, {}, {}, {}, {}

        def o_passes(m):
            j, i = divmod(m, ROW_TILES)
            o_bank[m] = psum.tile([P, KP], F32, name="o%d" % m, tag="acc", bufs=6)
            for g in range(KEY_PASSES):
                cols = slice(P * (2 * (i % 2) + g), P * (2 * (i % 2) + g + 1))
                nc.tensor.matmul_mx(
                    out=o_bank[m][:], lhsT=q_codes[i // 2][:, cols].bitcast(FP8X4), lhsT_scale=q_scales[i // 2][:, cols],
                    rhs=s_codes[j, g][:].bitcast(FP8X4), rhs_scale=s_scales[j, g][:],
                    start=(g == 0), stop=(g == KEY_PASSES - 1))

        def rows_of(store, m):
            j, i = divmod(m, ROW_TILES)
            return store[j, i // 4][:, KP * (i % 4):KP * (i % 4 + 1)]

        def silu_gate(m):
            silu[m] = work.tile([P, KP], F32, name="silu%d" % m, tag="silu", bufs=6)
            nc.scalar.activation(out=silu[m][:], in_=rows_of(gate_sb, m), func=ACT.Silu)

        def add_local(m):
            summed[m] = work.tile([P, KP], F32, name="summed%d" % m, tag="summed", bufs=3)
            nc.vector.tensor_tensor(out=summed[m][:], in0=o_bank[m][:], in1=rows_of(local_sb, m), op=ALU.add)

        def y_rows(m):
            return y_sb[m // 4][:, KP * (m % 4):KP * (m % 4 + 1)]

        def apply_gate(m, engine):
            if m % 4 == 0:
                y_sb[m // 4] = big("y%d" % (m // 4), F32)
            engine.tensor_tensor(out=y_rows(m), in0=summed[m][:], in1=silu[m][:], op=ALU.mult)

        def store_y(m0, count):
            j, i = divmod(m0, ROW_TILES)
            nc.sync.dma_start(
                out=out_0[P * i:P * (i + count), KP * j:KP * (j + 1)].rearrange("(i p) e -> p i e", p=P),
                in_=y_sb[m0 // 4][:, KP * (m0 % 4):KP * (m0 % 4 + count)].rearrange("p (i e) -> p i e", e=KP))

        def pool_copy(out, in_):
            nc.gpsimd.tensor_scalar(out=out, in0=in_, scalar1=1.0, scalar2=1.0, op0=ALU.mult, op1=ALU.mult)

        def round_y(m, copy):
            y_bf[m] = work.tile([P, KP], BF16, name="y_bf%d" % m, tag="y_bf", bufs=4)
            copy(out=y_bf[m][:].rearrange("p (u a e) -> p u a e", u=2, e=2),
                 in_=y_rows(m).rearrange("p (a u e) -> p u a e", u=2, e=2))

        def turn_y(m0, count):
            y_bank[m0] = psum.tile([P, KP], F32, name="y_bank%d" % m0, tag="turn", bufs=2)
            for b in range(count):
                words = y_bf[m0 + b][:].bitcast(F32)
                for u in range(2):
                    nc.tensor.transpose(y_bank[m0][:, P * (2 * b + u):P * (2 * b + u + 1)],
                                        words[:, P * u:P * (u + 1)], ident[:])

        def copy_y(m0, count, copy):
            y_mixed[m0] = work.tile([P, KP * count], BF16, name="y_mixed%d" % m0, tag="y_mixed", bufs=3, align_bytes=64)
            copy(out=y_mixed[m0][:].bitcast(F32).rearrange("p (b r u) -> p b r u", b=count, u=2),
                 in_=y_bank[m0][:, :2 * P * count].rearrange("p (b u r) -> p b r u", b=count, u=2))

        def quantize_y(m0, count):
            j, i = divmod(m0, ROW_TILES)
            if i == 0:
                y_codes[j] = work.tile([P, R], U32, name="y_codes%d" % j, tag="y_codes", bufs=2, align_bytes=64)
                y_scales[j] = keep.tile([P, R], U8, name="y_scales%d" % j, align_bytes=64)
            cols = slice(P * i, P * (i + count))
            nc.vector.quantize_mx(out=y_codes[j][:, cols].bitcast(FP8X4), scales=y_scales[j][:, cols],
                                  in_=y_mixed[m0][:])

        def store_codes(j, first, last):
            nc.sync.dma_start(out=out_1[j].rearrange("p m t -> p (m t)").bitcast(I32)[:, first:last],
                              in_=y_codes[j][:, first:last].bitcast(I32))

        def store_scales(j, queues):
            for quad in (0, 2, 1, 3):
                queues[quad % len(queues)].dma_start(out=out_2[j, 4 * quad:4 * quad + 4, :].bitcast(I32),
                                  in_=y_scales[j][32 * quad:32 * quad + 4, :].bitcast(I32))

        sort_x_scales(0, 0, 2)
        sort_x_codes(0, 0, 2)
        sort_x_scales(0, 2, 4)
        sort_x_codes(0, 2, 4)
        nc.vector.tensor_copy(out=decay_f[:], in_=decay_bf[:])
        h_passes(0, 0, 2)
        h_passes(1, 0, 2)
        h_passes(0, 2, 4)
        h_passes(1, 2, 4)
        h_passes(2, 0, 4)
        h_passes(3, 0, 4)
        for n in range(4):
            decay_state(n)
        sort_x_scales(1, 0, 4)
        sort_x_codes(1, 0, 2)
        form_s(0)
        h_passes(4, 0, 2)
        h_passes(5, 0, 2)
        sort_x_codes(1, 2, 4)
        form_s(1)
        form_s(2)
        form_s(3)
        for n in range(4, 8):
            decay_state(n)
            h_passes(n, 2 if n < 6 else 0, 4)
            if n == 7:
                mix_s(0, 0, 48)
            form_s(n)
        turn_q(0)
        turn_q(1)
        h_passes(8, 0, 4)
        copy_q(0)
        copy_q(1)
        turn_q(2)
        turn_q(3)
        quantize_s(0, 0)
        mix_s(0, 1, 128)
        quantize_q(0)
        quantize_s(0, 1)
        o_passes(0)
        decay_state(8)
        copy_q(2)
        copy_q(3)
        form_s(8)
        silu_gate(0)
        silu_gate(1)
        decay_state(9)
        silu_gate(2)
        silu_gate(3)

        last = OUT_UNITS - 1

        def state_unit(m):
            if m == 1:
                return 9
            if m in (0, 2) or m > 12:
                return None
            return m + 7 if m < 8 else m + 11

        for m in range(OUT_UNITS + 1):
            n = state_unit(m)
            if m == ROW_TILES:
                form_s(15)
                h_passes(16, 0, TOKEN_PASSES)
                h_passes(17, 0, TOKEN_PASSES)
                apply_gate(m - 1, nc.vector)
                mix_s(1, 1, 128)
                form_s(16)
                h_passes(18, 0, TOKEN_PASSES)
                decay_state(19)
                quantize_s(1, 1)
                o_passes(m)
                form_s(17)
                h_passes(19, 0, TOKEN_PASSES)
                form_s(18)
                decay_state(20)
            if m <= last:
                add_local(m)
            if m == 13:
                mix_s(2, 1, 40)
            if m >= 1 and m != ROW_TILES:
                apply_gate(m - 1, nc.vector)
            if m in (0, 2, 4):
                quantize_q(m // 2 + 1)
            if m in (7, 11):
                quantize_s(m // 4, 0)
            if m == 14:
                quantize_s(2, 1)
            if m % 2 == 0 and m >= 6:
                quantize_y(m - 6, 2)
            if n is not None:
                form_s(n)
            if m < last and m + 1 != ROW_TILES:
                o_passes(m + 1)
            after = 15 if m == 7 else state_unit(m + 1) if m != 1 else None
            if after is not None:
                h_passes(after, 0, TOKEN_PASSES)
            if m in (0, 2):
                turn_q(m + 4)
                turn_q(m + 5)
            if m % 2 == 0 and m >= 4 and m < last:
                turn_y(m - 4, 2)
            if m == 0 or 2 <= m <= 6:
                decay_state(10 if m == 0 else m + 9)
            if m == 7:
                for ahead in range(16, 19):
                    decay_state(ahead)
            if 8 <= m <= 10:
                decay_state(m + 13)
            if m in (5, 9):
                mix_s(m // 4, 0, 0)
            if m in (0, 2):
                copy_q(m + 4)
                copy_q(m + 5)
            if m + SILU_AHEAD <= last:
                silu_gate(m + SILU_AHEAD)
            if 1 <= m <= last:
                round_y(m - 1, pool_copy if m <= 12 else nc.scalar.copy)
            if m % 2 == 0 and m >= 4 and m < last:
                copy_y(m - 4, 2, nc.scalar.copy)
            if m % 2 == 0 and 2 <= m < last:
                store_y(m - 2, 2)
            if m >= last:
                store_y(m - 1, 1)
            if m % 4 == 0 and m >= 8:
                half = (m - 8) // 4
                store_codes(half // 2, KP * (half % 2), KP * (half % 2 + 1))
                if half % 2 == 1:
                    store_scales(half // 2, [nc.sync])
            if m == last:
                turn_y(last - 3, 2)
                copy_y(last - 3, 2, nc.scalar.copy)
                turn_y(last - 1, 1)
                copy_y(last - 1, 1, nc.scalar.copy)
        round_y(last, nc.vector.tensor_copy)
        quantize_y(last - 3, 2)
        turn_y(last, 1)
        quantize_y(last - 1, 1)
        store_codes(CHUNKS - 1, KP, R - P)
        copy_y(last, 1, nc.vector.tensor_copy)
        quantize_y(last, 1)
        store_codes(CHUNKS - 1, R - P, R)
        store_scales(CHUNKS - 1, [nc.scalar, nc.sync])
